import numpy as np
import ml_dtypes


def mxq(x, axis, fmt="e4m3"):
    dtype, down = {"e4m3": (ml_dtypes.float8_e4m3fn, 7), "e5m2": (ml_dtypes.float8_e5m2, 14)}[fmt]
    v = np.moveaxis(np.asarray(x, np.float32).astype(ml_dtypes.bfloat16).astype(np.float64), axis, -1)
    blocks = v.reshape(v.shape[:-1] + (-1, 32))
    amax = np.abs(blocks).max(-1, keepdims=True)
    byte = np.maximum(np.where(amax > 0, np.frexp(amax)[1] - 1 + 127, 0) - down, 1)
    scale = np.exp2(byte - 127.0)
    codes = (blocks / scale).astype(np.float32).astype(dtype).astype(np.float64)
    return np.moveaxis((codes * scale).reshape(v.shape), -1, axis)


WIDE = False


def mx_kscale(k):
    if not WIDE:
        return np.ones(k)
    levels = np.array([30, -30])
    if k % 512:
        return np.exp2(np.random.permutation(np.resize(levels, k // 32))).repeat(32)
    a = np.empty((k // 512, 16))
    for p in range(k // 512):
        a[p, :8] = np.random.permutation(np.resize(levels, 8))
        for g in range(8):
            far = levels[np.abs(levels - a[p, g]) >= 10]
            a[p, g + 8] = far[np.random.randint(len(far))]
    return np.exp2(a.ravel()).repeat(32)


def f64(x):
    return np.asarray(x).astype(np.float64)


def striped(idx):
    return np.tile(idx.reshape(-1, 16).T, (8, 1)).astype(np.uint16)


def unstriped(offs):
    return offs[:16].T.reshape(-1).astype(np.int64)


E2M1 = np.array([0.0, 0.5, 1.0, 1.5, 2.0, 3.0, 4.0, 6.0, -0.0, -0.5, -1.0, -1.5, -2.0, -3.0, -4.0, -6.0])


def pack_weight(w, fmt):
    k, n = w.shape
    w = f64(np.asarray(w, np.float32).astype(ml_dtypes.bfloat16)).reshape(k // 32, 32, n)
    amax = np.abs(w).max(1)
    if fmt == "e4m3":
        byte = np.frexp(amax)[1] - 1 + 127 - 7
    else:
        mant, ex = np.frexp(amax / 6.0)
        byte = np.where(mant > 0.5, ex, ex - 1) + 127
    byte = np.clip(np.where(amax > 0, byte, 1), 1, 254)
    scaled = (w * np.exp2(127.0 - byte)[:, None, :]).reshape(k, n).astype(np.float32)
    by_word = np.ascontiguousarray(scaled.reshape(k // 512, 128, 4, n).transpose(0, 1, 3, 2))
    if fmt == "e4m3":
        words = by_word.astype(ml_dtypes.float8_e4m3fn).view(np.uint8)
    else:
        c = by_word.astype(ml_dtypes.float4_e2m1fn).view(np.uint8) & 0xF
        words = (c[..., 0::2] | (c[..., 1::2] << 4)).reshape(k // 512, 128, 2 * n)
    return np.ascontiguousarray(words), np.ascontiguousarray(byte.astype(np.uint8).reshape(k // 512, 16, n))


def unpack_weight(words, scales, fmt):
    g, _, n = scales.shape
    words = np.ascontiguousarray(words).reshape(g, 128, n, -1)
    if fmt == "e4m3":
        vals = words.view(ml_dtypes.float8_e4m3fn).astype(np.float64)
    else:
        nib = np.empty((g, 128, n, 4), np.uint8)
        nib[..., 0::2] = words & 0xF
        nib[..., 1::2] = words >> 4
        vals = E2M1[nib]
    vals = vals * np.repeat(np.exp2(scales.astype(np.float64) - 127.0), 8, axis=1)[..., None]
    return vals.transpose(0, 1, 3, 2).reshape(g * 512, n)


def silu(v):
    return v / (1.0 + np.exp(-np.maximum(v, -700.0)))


def d_silu(v):
    s = 1.0 / (1.0 + np.exp(-np.maximum(v, -700.0)))
    return s * (1.0 + v * (1.0 - s))


K, T, E, C, H, N = 256, 1280, 2, 512, 512, 512


def by_expert(wq, xq):
    return np.concatenate([wq[e].T @ xq[:, e * C:(e + 1) * C] for e in range(E)], axis=1)


def setup_inputs():
    n = np.random.standard_normal
    s = mx_kscale(N)[:, None]
    u = mx_kscale(H)
    w2 = [pack_weight(m, "e2m1") for m in n((E, N, H)) / np.sqrt(N) / s[None] * u[None, None, :]]
    w1 = [pack_weight(m, "e2m1") for m in n((E, H, K)) / np.sqrt(H) / u[None, :, None]]
    w3 = [pack_weight(m, "e2m1") for m in n((E, H, K)) / np.sqrt(H) / u[None, :, None]]
    return {
        "dyT": (n((N, T)) * s).astype(np.float32),
        "a1": n((H, E * C)).astype(np.float32),
        "a3": n((H, E * C)).astype(np.float32),
        "w2_words": np.stack([m[0] for m in w2]),
        "w2_scales": np.stack([m[1] for m in w2]),
        "w1_words": np.stack([m[0] for m in w1]),
        "w1_scales": np.stack([m[1] for m in w1]),
        "w3_words": np.stack([m[0] for m in w3]),
        "w3_scales": np.stack([m[1] for m in w3]),
        "gate": np.tile(np.random.uniform(0.2, 1.0, E * C), (N, 1)).astype(np.float32),
        "offs": striped(np.random.permutation(T)[:E * C]),
    }


def reference(dyT, a1, a3, w2_words, w2_scales, w1_words, w1_scales, w3_words, w3_scales, gate, offs):
    idx = unstriped(offs)
    w2 = np.stack([unpack_weight(w2_words[e], w2_scales[e], "e2m1") for e in range(E)])
    w1 = np.stack([unpack_weight(w1_words[e], w1_scales[e], "e2m1") for e in range(E)])
    w3 = np.stack([unpack_weight(w3_words[e], w3_scales[e], "e2m1") for e in range(E)])
    gq = mxq(f64(gate) * f64(dyT)[:, idx], 0, "e5m2")
    dh = by_expert(w2, gq)
    da1 = dh * f64(a3) * d_silu(f64(a1))
    da3 = dh * silu(f64(a1))
    dx = by_expert(w1, mxq(da1, 0, "e5m2")) + by_expert(w3, mxq(da3, 0, "e5m2"))
    out = np.zeros((K, T))
    out[:, idx] = dx
    return out

@@ -1,0 +1,237 @@
+from contextlib import ExitStack
+
+import concourse.mybir as mybir
+
+K, T, E, C, H, N = 256, 1280, 2, 512, 512, 512
+S = E * C
+
+F32 = mybir.dt.float32
+BF16 = mybir.dt.bfloat16
+U32 = mybir.dt.uint32
+I32 = mybir.dt.int32
+U16 = mybir.dt.uint16
+U8 = mybir.dt.uint8
+E5M2X4 = mybir.dt.float8_e5m2_x4
+E2M1X4 = mybir.dt.float4_e2m1fn_x4
+ACT = mybir.ActivationFunctionType
+ALU = mybir.AluOpType
+
+P = 128
+J = 4
+
+FLOPS = 2 * S * (N * H + 2 * H * K)
+
+
+def tile_moe_bdx_glu_silu_kernel(
+    tc, dyT, a1, a3, w2_words, w2_scales, w1_words, w1_scales, w3_words, w3_scales, gate, offs, out
+):
+    nc = tc.nc
+    with ExitStack() as ctx:
+        lists = ctx.enter_context(tc.tile_pool(name="lists", bufs=1))
+        keep = ctx.enter_context(tc.tile_pool(name="keep", bufs=1))
+        psum = ctx.enter_context(tc.psum_pool(name="psum", bufs=1))
+
+        offsets = lists.tile([P, S // 16], U16, name="offsets")
+        nc.sync.dma_start(offsets[:], offs)
+
+        w2s_raw = keep.tile([P, E, H], U8, name="w2s_raw", align_bytes=64)
+        w1s = keep.tile([P, E, K], U8, name="w1s", align_bytes=64)
+        w3s = keep.tile([P, E, K], U8, name="w3s", align_bytes=64)
+        for plane in (w2s_raw, w1s, w3s):
+            nc.gpsimd.memset(plane[:].bitcast(I32), 0)
+        result = []
+        for kt in range(K // P):
+            res = keep.tile([P, T], F32, name=f"res{kt}")
+            result.append(res)
+
+        w2_raw = keep.tile([P, E, 2 * H], U8, name="w2_raw", align_bytes=64)
+        nc.sync.dma_start(w2_raw[:].bitcast(I32), w2_words.rearrange("e s p b -> p (e s) b").bitcast(I32))
+
+        dy = []
+        for t in range(J):
+            d = keep.tile([P, T], F32, name=f"dy{t}")
+            dy.append(d)
+        dy_rows = dyT.rearrange("(p t) w -> p t w", t=J)
+        gates = []
+        for e in range(E):
+            gt = keep.tile([P, C], F32, name=f"gate{e}")
+            gates.append(gt)
+        x1, x3 = [], []
+        for e in range(E):
+            a = keep.tile([P, J, C], F32, name=f"x1_{e}")
+            x1.append(a)
+            b = keep.tile([P, J, C], F32, name=f"x3_{e}")
+            x3.append(b)
+        a1_rows = a1.rearrange("(p t) c -> p t c", t=J)
+        a3_rows = a3.rearrange("(p t) c -> p t c", t=J)
+
+        def load_dy(t):
+            nc.sync.dma_start(dy[t][:], dy_rows[:, t, :])
+
+        def load_half(dst, rows, e, h):
+            nc.sync.dma_start(dst[e][:, 2 * h : 2 * h + 2, :], rows[:, 2 * h : 2 * h + 2, e * C : (e + 1) * C])
+
+        def load_scales(dst, src, queue):
+            for q in range(4):
+                queue.dma_start(
+                    dst[32 * q : 32 * q + 4, :, :].bitcast(I32),
+                    src[:, 0, 4 * q : 4 * q + 4, :].rearrange("e f n -> f e n").bitcast(I32),
+                )
+
+        load_dy(0)
+        for e in range(E):
+            nc.sync.dma_start(gates[e][:], gate[0:P, e * C : (e + 1) * C])
+        load_dy(1)
+        load_half(x1, a1_rows, 0, 0)
+        load_dy(2)
+        load_half(x1, a1_rows, 0, 1)
+        load_scales(w2s_raw, w2_scales, nc.sync)
+        load_dy(3)
+        for h in range(2):
+            load_half(x3, a3_rows, 0, h)
+        w1 = keep.tile([P, E, 2 * K], U8, name="w1", align_bytes=64)
+        w3 = keep.tile([P, E, 2 * K], U8, name="w3", align_bytes=64)
+        nc.sync.dma_start(w1[:].bitcast(I32), w1_words.rearrange("e s p b -> p (e s) b").bitcast(I32))
+        nc.sync.dma_start(w3[:].bitcast(I32), w3_words.rearrange("e s p b -> p (e s) b").bitcast(I32))
+        load_scales(w1s, w1_scales, nc.gpsimd)
+        load_scales(w3s, w3_scales, nc.gpsimd)
+        for kt in range(K // P):
+            nc.gpsimd.memset(result[kt][:], 0.0)
+        for h in range(2):
+            load_half(x1, a1_rows, 1, h)
+        for h in range(2):
+            load_half(x3, a3_rows, 1, h)
+
+        w2 = keep.tile([P, E, 2 * H], U8, name="w2", align_bytes=64)
+        w2s = keep.tile([P, E, H], U8, name="w2s", align_bytes=64)
+        nc.vector.tensor_copy(
+            w2[:].bitcast(U16).rearrange("p e (t m) -> p e t m", t=J),
+            w2_raw[:].bitcast(U16).rearrange("p e (m t) -> p e t m", t=J),
+        )
+
+        g4, g_bf, s, m, v, u, dh = [], [], [], [], [], [], []
+        for e in range(E):
+            for group, label, dtype, shape in (
+                (g4, "g4", F32, [P, J, C]),
+                (g_bf, "gbf", BF16, [P, C, J]),
+                (s, "s", F32, [P, J, C]),
+                (m, "m", F32, [P, J, C]),
+                (v, "v", F32, [P, J, C]),
+                (u, "u", F32, [P, J, C]),
+                (dh, "dh", F32, [P, J, C]),
+            ):
+                tl = keep.tile(shape, dtype, name=f"{label}_{e}", align_bytes=64)
+                group.append(tl)
+
+        def by4(tile4):
+            return tile4[:].rearrange("p t (c i) -> p c t i", i=4)
+
+        def by4_out(tile4):
+            return tile4[:].rearrange("p (c i) t -> p c t i", i=4)
+
+        def gather(e, t):
+            nc.vector.tensor_tensor(
+                g4[e][:, t, :], dy[t][:].indirect(offsets[:, 32 * e : 32 * e + 32]), gates[e][:], ALU.mult
+            )
+
+        def sig(e):
+            for h in range(2):
+                nc.scalar.activation(s[e][:, 2 * h : 2 * h + 2, :], x1[e][:, 2 * h : 2 * h + 2, :], ACT.Sigmoid)
+
+        def silu_neg(e):
+            for h in range(2):
+                cols = slice(h * 256, h * 256 + 256)
+                nc.scalar.activation(m[e][:, :, cols], x1[e][:, :, cols], ACT.Silu, scale=-1.0)
+
+        def make_u(e):
+            for h in range(2):
+                cols = slice(h * 256, h * 256 + 256)
+                nc.vector.scalar_tensor_tensor(
+                    s[e][:, :, cols], m[e][:, :, cols], 1.0, s[e][:, :, cols], ALU.subtract, ALU.mult
+                )
+            nc.vector.scalar_tensor_tensor(u[e][:], s[e][:], -1.0, x3[e][:], ALU.mult, ALU.mult)
+
+        def quantise(src, label):
+            codes = keep.tile([P, C], U32, name=f"codes_{label}", align_bytes=64)
+            scales = keep.tile([P, C], U8, name=f"scales_{label}", align_bytes=64)
+            nc.vector.quantize_mx(
+                out=codes[:].bitcast(E5M2X4), scales=scales[:], in_=src[:].rearrange("p c t -> p (c t)")
+            )
+            return codes, scales
+
+        def first_product(e, gq, gs):
+            for t in range(J):
+                acc = psum.tile([P, C], F32, name=f"dh_acc{t}")
+                nc.tensor.matmul_mx(
+                    out=acc[:],
+                    lhsT=w2[:, e, 256 * t : 256 * t + 256].bitcast(E2M1X4),
+                    lhsT_scale=w2s[:, e, 128 * t : 128 * t + 128],
+                    rhs=gq[:].bitcast(E5M2X4),
+                    rhs_scale=gs[:],
+                    start=True,
+                    stop=True,
+                )
+                nc.scalar.copy(dh[e][:, t, :], acc[:])
+
+        def make_da(e):
+            res = []
+            for factor, label in ((u, "da1"), (v, "da3")):
+                da = keep.tile([P, C, J], BF16, name=f"{label}_{e}", align_bytes=64)
+                nc.vector.tensor_tensor(by4_out(da), by4(dh[e]), by4(factor[e]), ALU.mult)
+                res.append(da)
+            return res
+
+        def second_product(e, kt, q1, q3):
+            acc = psum.tile([P, C], F32, name=f"dx_acc{kt}_{e}")
+            for n, (wt, ws, (codes, scales)) in enumerate(((w1, w1s, q1), (w3, w3s, q3))):
+                nc.tensor.matmul_mx(
+                    out=acc[:],
+                    lhsT=wt[:, e, 256 * kt : 256 * kt + 256].bitcast(E2M1X4),
+                    lhsT_scale=ws[:, e, 128 * kt : 128 * kt + 128],
+                    rhs=codes[:].bitcast(E5M2X4),
+                    rhs_scale=scales[:],
+                    start=(n == 0),
+                    stop=(n == 1),
+                )
+            dx = keep.tile([P, C], F32, name=f"dx{kt}_{e}")
+            nc.scalar.copy(dx[:], acc[:])
+            return dx
+
+        def scatter(e, kt, dx):
+            nc.vector.tensor_copy(result[kt][:].indirect(offsets[:, 32 * e : 32 * e + 32]), dx[:])
+
+        for e, t in ((0, 0), (1, 0), (0, 1), (1, 1), (0, 2), (0, 3)):
+            gather(e, t)
+        nc.vector.tensor_copy(
+            w2s[:].rearrange("p e (t m) -> p e t m", t=J),
+            w2s_raw[:].rearrange("p e (m t) -> p e t m", t=J),
+        )
+        sig(0)
+        silu_neg(0)
+        nc.scalar.copy(by4_out(g_bf[0]), by4(g4[0]))
+        make_u(0)
+        q0 = quantise(g_bf[0], "g0")
+        first_product(0, *q0)
+        nc.scalar.activation(v[0][:], x1[0][:], ACT.Silu)
+        gather(1, 2)
+        gather(1, 3)
+        da1, da3 = make_da(0)
+        q1 = quantise(da1, "da1_0")
+        q3 = quantise(da3, "da3_0")
+        silu_neg(1)
+        nc.scalar.copy(by4_out(g_bf[1]), by4(g4[1]))
+        sig(1)
+        dx0 = [second_product(0, kt, q1, q3) for kt in range(2)]
+        scatter(0, 0, dx0[0])
+        q0 = quantise(g_bf[1], "g1")
+        make_u(1)
+        first_product(1, *q0)
+        nc.scalar.activation(v[1][:], x1[1][:], ACT.Silu)
+        da1, da3 = make_da(1)
+        q1 = quantise(da1, "da1_1")
+        q3 = quantise(da3, "da3_1")
+        dx1 = [second_product(1, kt, q1, q3) for kt in range(2)]
+        scatter(0, 1, dx0[1])
+        for kt in range(2):
+            scatter(1, kt, dx1[kt])
+            nc.sync.dma_start(out[kt * P : (kt + 1) * P, :], result[kt][:])

@@ -45,83 +45,71 @@ def tile_moe_bdx_glu_silu_kernel(
             result.append(res)
 
         w2_raw = keep.tile([P, E, 2 * H], U8, name="w2_raw", align_bytes=64)
-        nc.sync.dma_start(w2_raw[:].bitcast(I32), w2_words.rearrange("e s p b -> p (e s) b").bitcast(I32))
-
+        w2 = keep.tile([P, E, 2 * H], U8, name="w2", align_bytes=64)
+        w2s = keep.tile([P, E, H], U8, name="w2s", align_bytes=64)
+        w1 = keep.tile([P, E, 2 * K], U8, name="w1", align_bytes=64)
+        w3 = keep.tile([P, E, 2 * K], U8, name="w3", align_bytes=64)
+        x1 = keep.tile([P, J, S], F32, name="x1")
+        x3 = keep.tile([P, J, S], F32, name="x3")
+        sg = keep.tile([P, J, S], F32, name="sg")
         dy = []
         for t in range(J):
             d = keep.tile([P, T], F32, name=f"dy{t}")
             dy.append(d)
         dy_rows = dyT.rearrange("(p t) w -> p t w", t=J)
-        gates = []
-        for e in range(E):
-            gt = keep.tile([P, C], F32, name=f"gate{e}")
-            gates.append(gt)
-        x1, x3 = [], []
-        for e in range(E):
-            a = keep.tile([P, J, C], F32, name=f"x1_{e}")
-            x1.append(a)
-            b = keep.tile([P, J, C], F32, name=f"x3_{e}")
-            x3.append(b)
         a1_rows = a1.rearrange("(p t) c -> p t c", t=J)
         a3_rows = a3.rearrange("(p t) c -> p t c", t=J)
-
-        def load_dy(t):
-            nc.sync.dma_start(dy[t][:], dy_rows[:, t, :])
-
-        def load_half(dst, rows, e, h):
-            nc.sync.dma_start(dst[e][:, 2 * h : 2 * h + 2, :], rows[:, 2 * h : 2 * h + 2, e * C : (e + 1) * C])
-
-        def load_scales(dst, src, queue):
-            for q in range(4):
-                queue.dma_start(
-                    dst[32 * q : 32 * q + 4, :, :].bitcast(I32),
-                    src[:, 0, 4 * q : 4 * q + 4, :].rearrange("e f n -> f e n").bitcast(I32),
-                )
-
-        load_dy(0)
-        for e in range(E):
-            nc.sync.dma_start(gates[e][:], gate[0:P, e * C : (e + 1) * C])
-        load_dy(1)
-        load_half(x1, a1_rows, 0, 0)
-        load_dy(2)
-        load_half(x1, a1_rows, 0, 1)
-        load_scales(w2s_raw, w2_scales, nc.sync)
-        load_dy(3)
-        for h in range(2):
-            load_half(x3, a3_rows, 0, h)
-        w1 = keep.tile([P, E, 2 * K], U8, name="w1", align_bytes=64)
-        w3 = keep.tile([P, E, 2 * K], U8, name="w3", align_bytes=64)
-        nc.sync.dma_start(w1[:].bitcast(I32), w1_words.rearrange("e s p b -> p (e s) b").bitcast(I32))
-        nc.sync.dma_start(w3[:].bitcast(I32), w3_words.rearrange("e s p b -> p (e s) b").bitcast(I32))
-        load_scales(w1s, w1_scales, nc.gpsimd)
-        load_scales(w3s, w3_scales, nc.gpsimd)
-        for kt in range(K // P):
-            nc.gpsimd.memset(result[kt][:], 0.0)
-        for h in range(2):
-            load_half(x1, a1_rows, 1, h)
-        for h in range(2):
-            load_half(x3, a3_rows, 1, h)
-
-        w2 = keep.tile([P, E, 2 * H], U8, name="w2", align_bytes=64)
-        w2s = keep.tile([P, E, H], U8, name="w2s", align_bytes=64)
-        nc.vector.tensor_copy(
-            w2[:].bitcast(U16).rearrange("p e (t m) -> p e t m", t=J),
-            w2_raw[:].bitcast(U16).rearrange("p e (m t) -> p e t m", t=J),
-        )
-
-        g4, g_bf, s, m, v, u, dh = [], [], [], [], [], [], []
+        gates, g4, m, u, dh = [], [], [], [], []
         for e in range(E):
             for group, label, dtype, shape in (
+                (gates, "gate", F32, [P, C]),
                 (g4, "g4", F32, [P, J, C]),
-                (g_bf, "gbf", BF16, [P, C, J]),
-                (s, "s", F32, [P, J, C]),
                 (m, "m", F32, [P, J, C]),
-                (v, "v", F32, [P, J, C]),
                 (u, "u", F32, [P, J, C]),
                 (dh, "dh", F32, [P, J, C]),
             ):
                 tl = keep.tile(shape, dtype, name=f"{label}_{e}", align_bytes=64)
                 group.append(tl)
+        g_bf, v, codes, planes, da, acc1, acc2, dxs = {}, {}, {}, {}, {}, {}, {}, {}
+
+        def planes_of(h):
+            return slice(2 * h, 2 * h + 2)
+
+        def cols_of(e, h):
+            return slice(e * C + 256 * h, e * C + 256 * h + 256)
+
+        def load_dy(t):
+            nc.sync.dma_start(dy[t][:], dy_rows[:, t, :])
+
+        def load_gate(e):
+            nc.sync.dma_start(gates[e][:], gate[0:P, e * C : (e + 1) * C])
+
+        def load_half(dst, rows, h):
+            nc.sync.dma_start(dst[:, planes_of(h), :], rows[:, planes_of(h), :])
+
+        def load_scales(dst, src, q):
+            nc.sync.dma_start(
+                dst[32 * q : 32 * q + 4, :, :].bitcast(I32),
+                src[:, 0, 4 * q : 4 * q + 4, :].rearrange("e f n -> f e n").bitcast(I32),
+            )
+
+        def load_words(dst, src):
+            nc.sync.dma_start(dst[:].bitcast(I32), src.rearrange("e s p b -> p (e s) b").bitcast(I32))
+
+        def permute_words():
+            nc.vector.tensor_copy(
+                w2[:].bitcast(U16).rearrange("p e (t m) -> p e t m", t=J),
+                w2_raw[:].bitcast(U16).rearrange("p e (m t) -> p e t m", t=J),
+            )
+
+        def permute_scales():
+            nc.vector.tensor_copy(
+                w2s[:].rearrange("p e (t m) -> p e t m", t=J),
+                w2s_raw[:].rearrange("p e (m t) -> p e t m", t=J),
+            )
+
+        def slots(e):
+            return offsets[:, 32 * e : 32 * e + 32]
 
         def by4(tile4):
             return tile4[:].rearrange("p t (c i) -> p c t i", i=4)
@@ -130,108 +118,181 @@ def tile_moe_bdx_glu_silu_kernel(
             return tile4[:].rearrange("p (c i) t -> p c t i", i=4)
 
         def gather(e, t):
-            nc.vector.tensor_tensor(
-                g4[e][:, t, :], dy[t][:].indirect(offsets[:, 32 * e : 32 * e + 32]), gates[e][:], ALU.mult
+            nc.vector.tensor_tensor(g4[e][:, t, :], dy[t][:].indirect(slots(e)), gates[e][:], ALU.mult)
+
+        def sig(h):
+            nc.scalar.activation(sg[:, planes_of(h), :], x1[:, planes_of(h), :], ACT.Sigmoid)
+
+        def silu_neg(e, h):
+            nc.scalar.activation(
+                m[e][:, :, 256 * h : 256 * h + 256], x1[:, :, cols_of(e, h)], ACT.Silu, scale=-1.0
             )
 
-        def sig(e):
-            for h in range(2):
-                nc.scalar.activation(s[e][:, 2 * h : 2 * h + 2, :], x1[e][:, 2 * h : 2 * h + 2, :], ACT.Sigmoid)
+        def silu(e):
+            o = keep.tile([P, J, C], F32, name=f"v_{e}", align_bytes=64)
+            nc.scalar.activation(o[:], x1[:, :, e * C : (e + 1) * C], ACT.Silu)
+            v[e] = o
 
-        def silu_neg(e):
-            for h in range(2):
-                cols = slice(h * 256, h * 256 + 256)
-                nc.scalar.activation(m[e][:, :, cols], x1[e][:, :, cols], ACT.Silu, scale=-1.0)
+        def interleave(e):
+            o = keep.tile([P, C, J], BF16, name="g_bf", align_bytes=64)
+            nc.scalar.copy(by4_out(o), by4(g4[e]))
+            g_bf[e] = o
 
-        def make_u(e):
-            for h in range(2):
-                cols = slice(h * 256, h * 256 + 256)
-                nc.vector.scalar_tensor_tensor(
-                    s[e][:, :, cols], m[e][:, :, cols], 1.0, s[e][:, :, cols], ALU.subtract, ALU.mult
-                )
-            nc.vector.scalar_tensor_tensor(u[e][:], s[e][:], -1.0, x3[e][:], ALU.mult, ALU.mult)
+        def make_p(t):
+            nc.vector.scalar_tensor_tensor(sg[:, t, :], sg[:, t, :], -1.0, x3[:, t, :], ALU.mult, ALU.mult)
+
+        def make_u(e, h):
+            c = slice(256 * h, 256 * h + 256)
+            nc.vector.scalar_tensor_tensor(
+                u[e][:, :, c], m[e][:, :, c], 1.0, sg[:, :, cols_of(e, h)], ALU.subtract, ALU.mult
+            )
 
         def quantise(src, label):
-            codes = keep.tile([P, C], U32, name=f"codes_{label}", align_bytes=64)
-            scales = keep.tile([P, C], U8, name=f"scales_{label}", align_bytes=64)
-            nc.vector.quantize_mx(
-                out=codes[:].bitcast(E5M2X4), scales=scales[:], in_=src[:].rearrange("p c t -> p (c t)")
+            q = keep.tile([P, C], U32, name=f"codes_{label}", align_bytes=64)
+            z = keep.tile([P, C], U8, name=f"scales_{label}", align_bytes=64)
+            nc.vector.quantize_mx(out=q[:].bitcast(E5M2X4), scales=z[:], in_=src[:].rearrange("p c t -> p (c t)"))
+            codes[label], planes[label] = q, z
+
+        def first_product(e, t):
+            acc = psum.tile([P, C], F32, name=f"dh_acc{t}")
+            nc.tensor.matmul_mx(
+                out=acc[:],
+                lhsT=w2[:, e, 256 * t : 256 * t + 256].bitcast(E2M1X4),
+                lhsT_scale=w2s[:, e, 128 * t : 128 * t + 128],
+                rhs=codes[f"g{e}"][:].bitcast(E5M2X4),
+                rhs_scale=planes[f"g{e}"][:],
+                start=True,
+                stop=True,
             )
-            return codes, scales
+            acc1[e, t] = acc
 
-        def first_product(e, gq, gs):
-            for t in range(J):
-                acc = psum.tile([P, C], F32, name=f"dh_acc{t}")
-                nc.tensor.matmul_mx(
-                    out=acc[:],
-                    lhsT=w2[:, e, 256 * t : 256 * t + 256].bitcast(E2M1X4),
-                    lhsT_scale=w2s[:, e, 128 * t : 128 * t + 128],
-                    rhs=gq[:].bitcast(E5M2X4),
-                    rhs_scale=gs[:],
-                    start=True,
-                    stop=True,
-                )
-                nc.scalar.copy(dh[e][:, t, :], acc[:])
+        def copy_dh(e, t):
+            nc.scalar.copy(dh[e][:, t, :], acc1[e, t][:])
 
-        def make_da(e):
-            res = []
-            for factor, label in ((u, "da1"), (v, "da3")):
-                da = keep.tile([P, C, J], BF16, name=f"{label}_{e}", align_bytes=64)
-                nc.vector.tensor_tensor(by4_out(da), by4(dh[e]), by4(factor[e]), ALU.mult)
-                res.append(da)
-            return res
+        def make_da(label, e, factor):
+            o = keep.tile([P, C, J], BF16, name=f"da{label}_{e}", align_bytes=64)
+            nc.vector.tensor_tensor(by4_out(o), by4(dh[e]), by4(factor), ALU.mult)
+            da[label, e] = o
 
-        def second_product(e, kt, q1, q3):
+        def second_product(e, kt):
             acc = psum.tile([P, C], F32, name=f"dx_acc{kt}_{e}")
-            for n, (wt, ws, (codes, scales)) in enumerate(((w1, w1s, q1), (w3, w3s, q3))):
+            for n, (wt, ws, label) in enumerate(((w1, w1s, f"da1_{e}"), (w3, w3s, f"da3_{e}"))):
                 nc.tensor.matmul_mx(
                     out=acc[:],
                     lhsT=wt[:, e, 256 * kt : 256 * kt + 256].bitcast(E2M1X4),
                     lhsT_scale=ws[:, e, 128 * kt : 128 * kt + 128],
-                    rhs=codes[:].bitcast(E5M2X4),
-                    rhs_scale=scales[:],
+                    rhs=codes[label][:].bitcast(E5M2X4),
+                    rhs_scale=planes[label][:],
                     start=(n == 0),
                     stop=(n == 1),
                 )
-            dx = keep.tile([P, C], F32, name=f"dx{kt}_{e}")
-            nc.scalar.copy(dx[:], acc[:])
-            return dx
+            acc2[e, kt] = acc
 
-        def scatter(e, kt, dx):
-            nc.vector.tensor_copy(result[kt][:].indirect(offsets[:, 32 * e : 32 * e + 32]), dx[:])
+        def copy_dx(e, kt):
+            tag = "v_1" if (e, kt) == (0, 1) else f"dx{kt}_{e}"
+            o = keep.tile([P, C], F32, name=f"dx{kt}_{e}", tag=tag, align_bytes=64)
+            nc.scalar.copy(o[:], acc2[e, kt][:])
+            dxs[e, kt] = o
 
-        for e, t in ((0, 0), (1, 0), (0, 1), (1, 1), (0, 2), (0, 3)):
-            gather(e, t)
-        nc.vector.tensor_copy(
-            w2s[:].rearrange("p e (t m) -> p e t m", t=J),
-            w2s_raw[:].rearrange("p e (m t) -> p e t m", t=J),
-        )
-        sig(0)
-        silu_neg(0)
-        nc.scalar.copy(by4_out(g_bf[0]), by4(g4[0]))
-        make_u(0)
-        q0 = quantise(g_bf[0], "g0")
-        first_product(0, *q0)
-        nc.scalar.activation(v[0][:], x1[0][:], ACT.Silu)
-        gather(1, 2)
-        gather(1, 3)
-        da1, da3 = make_da(0)
-        q1 = quantise(da1, "da1_0")
-        q3 = quantise(da3, "da3_0")
-        silu_neg(1)
-        nc.scalar.copy(by4_out(g_bf[1]), by4(g4[1]))
-        sig(1)
-        dx0 = [second_product(0, kt, q1, q3) for kt in range(2)]
-        scatter(0, 0, dx0[0])
-        q0 = quantise(g_bf[1], "g1")
-        make_u(1)
-        first_product(1, *q0)
-        nc.scalar.activation(v[1][:], x1[1][:], ACT.Silu)
-        da1, da3 = make_da(1)
-        q1 = quantise(da1, "da1_1")
-        q3 = quantise(da3, "da3_1")
-        dx1 = [second_product(1, kt, q1, q3) for kt in range(2)]
-        scatter(0, 1, dx0[1])
-        for kt in range(2):
-            scatter(1, kt, dx1[kt])
+        def scatter(e, kt):
+            nc.vector.tensor_copy(result[kt][:].indirect(slots(e)), dxs[e, kt][:])
+
+        def store(kt):
             nc.sync.dma_start(out[kt * P : (kt + 1) * P, :], result[kt][:])
+
+        for kt in range(K // P):
+            nc.gpsimd.memset(result[kt][:], 0.0)
+
+        load_dy(2)
+        load_dy(0)
+        load_words(w2_raw, w2_words)
+        load_gate(1)
+        load_half(x1, a1_rows, 0)
+        permute_words()
+        load_gate(0)
+        gather(1, 0)
+        load_dy(3)
+        gather(1, 2)
+        load_half(x1, a1_rows, 1)
+        sig(0)
+        gather(0, 0)
+        load_scales(w2s_raw, w2_scales, 0)
+        load_scales(w2s_raw, w2_scales, 1)
+        load_scales(w2s_raw, w2_scales, 2)
+        load_scales(w2s_raw, w2_scales, 3)
+        gather(0, 2)
+        load_dy(1)
+        gather(0, 3)
+        load_words(w3, w3_words)
+        load_half(x3, a3_rows, 0)
+        sig(1)
+        gather(1, 3)
+        permute_scales()
+        load_half(x3, a3_rows, 1)
+        gather(0, 1)
+        silu_neg(1, 1)
+        gather(1, 1)
+        load_words(w1, w1_words)
+        make_p(0)
+        interleave(0)
+        make_p(1)
+        load_scales(w1s, w1_scales, 3)
+        make_p(2)
+        load_scales(w3s, w3_scales, 1)
+        load_scales(w1s, w1_scales, 0)
+        load_scales(w1s, w1_scales, 1)
+        load_scales(w3s, w3_scales, 2)
+        load_scales(w1s, w1_scales, 2)
+        load_scales(w3s, w3_scales, 3)
+        load_scales(w3s, w3_scales, 0)
+        silu_neg(1, 0)
+        quantise(g_bf[0], "g0")
+        make_p(3)
+        silu_neg(0, 0)
+        first_product(0, 1)
+        first_product(0, 3)
+        first_product(0, 2)
+        first_product(0, 0)
+        make_u(1, 0)
+        silu_neg(0, 1)
+        make_u(0, 0)
+        copy_dh(0, 1)
+        copy_dh(0, 2)
+        make_u(0, 1)
+        copy_dh(0, 3)
+        interleave(1)
+        make_u(1, 1)
+        copy_dh(0, 0)
+        quantise(g_bf[1], "g1")
+        silu(0)
+        make_da("1", 0, u[0])
+        first_product(1, 0)
+        first_product(1, 1)
+        first_product(1, 2)
+        first_product(1, 3)
+        copy_dh(1, 0)
+        make_da("3", 0, v[0])
+        copy_dh(1, 3)
+        copy_dh(1, 1)
+        copy_dh(1, 2)
+        silu(1)
+        quantise(da["1", 0], "da1_0")
+        quantise(da["3", 0], "da3_0")
+        make_da("1", 1, u[1])
+        second_product(0, 0)
+        second_product(0, 1)
+        copy_dx(0, 0)
+        scatter(0, 0)
+        make_da("3", 1, v[1])
+        quantise(da["1", 1], "da1_1")
+        copy_dx(0, 1)
+        quantise(da["3", 1], "da3_1")
+        scatter(0, 1)
+        second_product(1, 0)
+        second_product(1, 1)
+        copy_dx(1, 0)
+        copy_dx(1, 1)
+        scatter(1, 0)
+        scatter(1, 1)
+        store(0)
+        store(1)

@@ -49,7 +49,7 @@ def tile_moe_bdx_glu_silu_kernel(
         w2s = keep.tile([P, E, H], U8, name="w2s", align_bytes=64)
         w1 = keep.tile([P, E, 2 * K], U8, name="w1", align_bytes=64)
         w3 = keep.tile([P, E, 2 * K], U8, name="w3", align_bytes=64)
-        x1 = keep.tile([P, J, S], F32, name="x1")
+        x1 = keep.tile([P, J, S], F32, name="x1", align_bytes=64)
         x3 = keep.tile([P, J, S], F32, name="x3")
         sg = keep.tile([P, J, S], F32, name="sg")
         dy = []
@@ -83,6 +83,9 @@ def tile_moe_bdx_glu_silu_kernel(
 
         def load_gate(e):
             nc.sync.dma_start(gates[e][:], gate[0:P, e * C : (e + 1) * C])
+
+        def load_plane(dst, rows, t):
+            nc.sync.dma_start(dst[:, t, :], rows[:, t, :])
 
         def load_half(dst, rows, h):
             nc.sync.dma_start(dst[:, planes_of(h), :], rows[:, planes_of(h), :])
@@ -120,8 +123,8 @@ def tile_moe_bdx_glu_silu_kernel(
         def gather(e, t):
             nc.vector.tensor_tensor(g4[e][:, t, :], dy[t][:].indirect(slots(e)), gates[e][:], ALU.mult)
 
-        def sig(h):
-            nc.scalar.activation(sg[:, planes_of(h), :], x1[:, planes_of(h), :], ACT.Sigmoid)
+        def sig(t):
+            nc.scalar.activation(sg[:, t, :], x1[:, t, :], ACT.Sigmoid)
 
         def silu_neg(e, h):
             nc.scalar.activation(
@@ -138,14 +141,45 @@ def tile_moe_bdx_glu_silu_kernel(
             nc.scalar.copy(by4_out(o), by4(g4[e]))
             g_bf[e] = o
 
-        def make_p(t):
-            nc.vector.scalar_tensor_tensor(sg[:, t, :], sg[:, t, :], -1.0, x3[:, t, :], ALU.mult, ALU.mult)
+        ps = {}
+
+        def make_p(e, h):
+            if e not in ps:
+                o = keep.tile([P, J, C], F32, name=f"p_{e}", align_bytes=64)
+                ps[e] = o
+            t, c = planes_of(h), slice(e * C, e * C + C)
+            if e == 1 and False:
+                nc.gpsimd.tensor_tensor(ps[e][:, t, :], sg[:, t, c], x3[:, t, c], ALU.mult)
+            else:
+                nc.vector.scalar_tensor_tensor(ps[e][:, t, :], sg[:, t, c], -1.0, x3[:, t, c], ALU.mult, ALU.mult)
+
+        def make_n(h):
+            c = slice(256 * h, 256 * h + 256)
+            nc.scalar.activation(m[1][:, :, c], m[1][:, :, c], ACT.Copy, bias=1.0, scale=-1.0)
 
         def make_u(e, h):
             c = slice(256 * h, 256 * h + 256)
-            nc.vector.scalar_tensor_tensor(
-                u[e][:, :, c], m[e][:, :, c], 1.0, sg[:, :, cols_of(e, h)], ALU.subtract, ALU.mult
-            )
+            if e == 1 and False:
+                nc.gpsimd.tensor_tensor(u[e][:, :, c], m[e][:, :, c], ps[e][:, :, c], ALU.mult)
+            else:
+                nc.vector.scalar_tensor_tensor(
+                    u[e][:, :, c], m[e][:, :, c], 1.0, ps[e][:, :, c], ALU.subtract, ALU.mult
+                )
+
+        daf = {}
+
+        def make_da_plane(label, e, t, factor):
+            if (label, e) not in daf:
+                name = f"daf{label}_{e}"
+                tag = {"daf3_1": "g4_0", "daf1_1": "g4_1"}.get(name, name)
+                o = keep.tile([P, J, C], F32, name=name, tag=tag, align_bytes=64)
+                daf[label, e] = o
+            nc.vector.tensor_tensor(daf[label, e][:, t, :], acc1[e, t][:], factor[:, t, :], ALU.mult)
+
+        def interleave_da(label, e):
+            o = keep.tile([P, C, J], BF16, name=f"da{label}_{e}", align_bytes=64)
+            nc.scalar.copy(by4_out(o), by4(daf[label, e]))
+            da[label, e] = o
 
         def quantise(src, label):
             q = keep.tile([P, C], U32, name=f"codes_{label}", align_bytes=64)
@@ -154,7 +188,7 @@ def tile_moe_bdx_glu_silu_kernel(
             codes[label], planes[label] = q, z
 
         def first_product(e, t):
-            acc = psum.tile([P, C], F32, name=f"dh_acc{t}")
+            acc = psum.tile([P, C], F32, name=f"dh_acc{t}_{e}")
             nc.tensor.matmul_mx(
                 out=acc[:],
                 lhsT=w2[:, e, 256 * t : 256 * t + 256].bitcast(E2M1X4),
@@ -175,7 +209,7 @@ def tile_moe_bdx_glu_silu_kernel(
             da[label, e] = o
 
         def second_product(e, kt):
-            acc = psum.tile([P, C], F32, name=f"dx_acc{kt}_{e}")
+            acc = psum.tile([P, C], F32, name=f"dx_acc{kt}_{e}", tag=f"dh_acc{kt + 2 * e}_0")
             for n, (wt, ws, label) in enumerate(((w1, w1s, f"da1_{e}"), (w3, w3s, f"da3_{e}"))):
                 nc.tensor.matmul_mx(
                     out=acc[:],
@@ -189,7 +223,7 @@ def tile_moe_bdx_glu_silu_kernel(
             acc2[e, kt] = acc
 
         def copy_dx(e, kt):
-            tag = "v_1" if (e, kt) == (0, 1) else f"dx{kt}_{e}"
+            tag = f"dx{kt}_{e}"
             o = keep.tile([P, C], F32, name=f"dx{kt}_{e}", tag=tag, align_bytes=64)
             nc.scalar.copy(o[:], acc2[e, kt][:])
             dxs[e, kt] = o
@@ -203,78 +237,82 @@ def tile_moe_bdx_glu_silu_kernel(
         for kt in range(K // P):
             nc.gpsimd.memset(result[kt][:], 0.0)
 
-        load_dy(2)
-        load_dy(0)
-        load_words(w2_raw, w2_words)
-        load_gate(1)
-        load_half(x1, a1_rows, 0)
-        permute_words()
         load_gate(0)
-        gather(1, 0)
-        load_dy(3)
-        gather(1, 2)
-        load_half(x1, a1_rows, 1)
-        sig(0)
-        gather(0, 0)
+        load_gate(1)
+        load_dy(2)
+        load_plane(x1, a1_rows, 0)
         load_scales(w2s_raw, w2_scales, 0)
         load_scales(w2s_raw, w2_scales, 1)
         load_scales(w2s_raw, w2_scales, 2)
         load_scales(w2s_raw, w2_scales, 3)
+        load_plane(x1, a1_rows, 3)
+        load_dy(3)
         gather(0, 2)
+        sig(0)
+        gather(1, 2)
+        load_words(w2_raw, w2_words)
         load_dy(1)
-        gather(0, 3)
-        load_words(w3, w3_words)
-        load_half(x3, a3_rows, 0)
-        sig(1)
-        gather(1, 3)
         permute_scales()
+        load_plane(x1, a1_rows, 1)
+        gather(1, 3)
+        sig(3)
+        load_plane(x1, a1_rows, 2)
+        permute_words()
+        load_dy(0)
+        gather(0, 3)
         load_half(x3, a3_rows, 1)
-        gather(0, 1)
-        silu_neg(1, 1)
         gather(1, 1)
+        sig(1)
+        sig(2)
+        gather(0, 1)
         load_words(w1, w1_words)
-        make_p(0)
+        load_half(x3, a3_rows, 0)
+        silu_neg(1, 0)
+        gather(0, 0)
+        gather(1, 0)
+        load_words(w3, w3_words)
+        make_p(0, 1)
+        silu_neg(1, 1)
+        make_p(1, 1)
         interleave(0)
-        make_p(1)
-        load_scales(w1s, w1_scales, 3)
-        make_p(2)
-        load_scales(w3s, w3_scales, 1)
+        make_p(0, 0)
         load_scales(w1s, w1_scales, 0)
         load_scales(w1s, w1_scales, 1)
-        load_scales(w3s, w3_scales, 2)
         load_scales(w1s, w1_scales, 2)
-        load_scales(w3s, w3_scales, 3)
+        load_scales(w1s, w1_scales, 3)
         load_scales(w3s, w3_scales, 0)
-        silu_neg(1, 0)
-        quantise(g_bf[0], "g0")
-        make_p(3)
+        load_scales(w3s, w3_scales, 1)
+        load_scales(w3s, w3_scales, 2)
+        load_scales(w3s, w3_scales, 3)
+        make_p(1, 0)
         silu_neg(0, 0)
-        first_product(0, 1)
-        first_product(0, 3)
+        quantise(g_bf[0], "g0")
+        silu_neg(0, 1)
+        make_u(1, 1)
         first_product(0, 2)
+        first_product(0, 3)
+        interleave(1)
+        first_product(0, 1)
         first_product(0, 0)
         make_u(1, 0)
-        silu_neg(0, 1)
         make_u(0, 0)
-        copy_dh(0, 1)
-        copy_dh(0, 2)
-        make_u(0, 1)
         copy_dh(0, 3)
-        interleave(1)
-        make_u(1, 1)
-        copy_dh(0, 0)
         quantise(g_bf[1], "g1")
+        copy_dh(0, 2)
+        copy_dh(0, 0)
+        make_u(0, 1)
+        first_product(1, 2)
+        first_product(1, 0)
+        copy_dh(0, 1)
+        first_product(1, 1)
+        first_product(1, 3)
         silu(0)
         make_da("1", 0, u[0])
-        first_product(1, 0)
-        first_product(1, 1)
-        first_product(1, 2)
-        first_product(1, 3)
         copy_dh(1, 0)
         make_da("3", 0, v[0])
-        copy_dh(1, 3)
         copy_dh(1, 1)
         copy_dh(1, 2)
+        copy_dh(1, 3)
         silu(1)
         quantise(da["1", 0], "da1_0")
         quantise(da["3", 0], "da3_0")
@@ -282,17 +320,17 @@ def tile_moe_bdx_glu_silu_kernel(
         second_product(0, 0)
         second_product(0, 1)
         copy_dx(0, 0)
-        scatter(0, 0)
-        make_da("3", 1, v[1])
-        quantise(da["1", 1], "da1_1")
         copy_dx(0, 1)
-        quantise(da["3", 1], "da3_1")
+        make_da("3", 1, v[1])
         scatter(0, 1)
-        second_product(1, 0)
+        quantise(da["3", 1], "da3_1")
+        quantise(da["1", 1], "da1_1")
+        scatter(0, 0)
         second_product(1, 1)
-        copy_dx(1, 0)
+        second_product(1, 0)
         copy_dx(1, 1)
-        scatter(1, 0)
+        copy_dx(1, 0)
         scatter(1, 1)
-        store(0)
+        scatter(1, 0)
         store(1)
+        store(0)

@@ -18,6 +18,9 @@ ALU = mybir.AluOpType
 
 P = 128
 J = 4
+LIST_COLS = C // 16
+QUADRANTS = 4
+RUN = 4
 
 FLOPS = 2 * S * (N * H + 2 * H * K)
 
@@ -34,303 +37,212 @@ def tile_moe_bdx_glu_silu_kernel(
         offsets = lists.tile([P, S // 16], U16, name="offsets")
         nc.sync.dma_start(offsets[:], offs)
 
-        w2s_raw = keep.tile([P, E, H], U8, name="w2s_raw", align_bytes=64)
-        w1s = keep.tile([P, E, K], U8, name="w1s", align_bytes=64)
-        w3s = keep.tile([P, E, K], U8, name="w3s", align_bytes=64)
-        for plane in (w2s_raw, w1s, w3s):
-            nc.gpsimd.memset(plane[:].bitcast(I32), 0)
+        def slots(e):
+            return offsets[:, e * LIST_COLS : (e + 1) * LIST_COLS]
+
+        def columns(e):
+            return slice(e * C, (e + 1) * C)
+
+        w2_scales_raw = keep.tile([P, E, H], U8, name="w2_scales_raw", align_bytes=64)
+        w1_sc = keep.tile([P, E, K], U8, name="w1_sc", align_bytes=64)
+        w3_sc = keep.tile([P, E, K], U8, name="w3_sc", align_bytes=64)
+        for scale_tile in (w2_scales_raw, w1_sc, w3_sc):
+            nc.gpsimd.memset(scale_tile[:].bitcast(I32), 0)
+
         result = []
         for kt in range(K // P):
-            res = keep.tile([P, T], F32, name=f"res{kt}")
-            result.append(res)
+            tile = keep.tile([P, T], F32, name=f"result{kt}")
+            nc.gpsimd.memset(tile[:], 0.0)
+            result.append(tile)
 
+        dy, gates = [], []
+        for t in range(J):
+            tile = keep.tile([P, T], F32, name=f"dy{t}")
+            dy.append(tile)
+        for e in range(E):
+            tile = keep.tile([P, C], F32, name=f"gate{e}")
+            gates.append(tile)
+        x1 = keep.tile([P, J, S], F32, name="x1", align_bytes=64)
+        x3 = keep.tile([P, J, S], F32, name="x3", align_bytes=64)
         w2_raw = keep.tile([P, E, 2 * H], U8, name="w2_raw", align_bytes=64)
-        w2 = keep.tile([P, E, 2 * H], U8, name="w2", align_bytes=64)
-        w2s = keep.tile([P, E, H], U8, name="w2s", align_bytes=64)
         w1 = keep.tile([P, E, 2 * K], U8, name="w1", align_bytes=64)
         w3 = keep.tile([P, E, 2 * K], U8, name="w3", align_bytes=64)
-        x1 = keep.tile([P, J, S], F32, name="x1", align_bytes=64)
-        x3 = keep.tile([P, J, S], F32, name="x3")
-        sg = keep.tile([P, J, S], F32, name="sg")
-        dy = []
-        for t in range(J):
-            d = keep.tile([P, T], F32, name=f"dy{t}")
-            dy.append(d)
         dy_rows = dyT.rearrange("(p t) w -> p t w", t=J)
         a1_rows = a1.rearrange("(p t) c -> p t c", t=J)
         a3_rows = a3.rearrange("(p t) c -> p t c", t=J)
-        gates, g4, m, u, dh = [], [], [], [], []
-        for e in range(E):
-            for group, label, dtype, shape in (
-                (gates, "gate", F32, [P, C]),
-                (g4, "g4", F32, [P, J, C]),
-                (m, "m", F32, [P, J, C]),
-                (u, "u", F32, [P, J, C]),
-                (dh, "dh", F32, [P, J, C]),
-            ):
-                tl = keep.tile(shape, dtype, name=f"{label}_{e}", align_bytes=64)
-                group.append(tl)
-        g_bf, v, codes, planes, da, acc1, acc2, dxs = {}, {}, {}, {}, {}, {}, {}, {}
-
-        def planes_of(h):
-            return slice(2 * h, 2 * h + 2)
-
-        def cols_of(e, h):
-            return slice(e * C + 256 * h, e * C + 256 * h + 256)
 
         def load_dy(t):
             nc.sync.dma_start(dy[t][:], dy_rows[:, t, :])
 
-        def load_gate(e):
-            nc.sync.dma_start(gates[e][:], gate[0:P, e * C : (e + 1) * C])
+        def load_a1(t):
+            nc.sync.dma_start(x1[:, t, :], a1_rows[:, t, :])
 
-        def load_plane(dst, rows, t):
-            nc.sync.dma_start(dst[:, t, :], rows[:, t, :])
+        def load_a3(half):
+            planes = slice(2 * half, 2 * half + 2)
+            nc.sync.dma_start(x3[:, planes, :], a3_rows[:, planes, :])
 
-        def load_half(dst, rows, h):
-            nc.sync.dma_start(dst[:, planes_of(h), :], rows[:, planes_of(h), :])
+        def load_words(tile, words):
+            nc.sync.dma_start(tile[:].bitcast(I32), words.rearrange("e s p b -> p (e s) b").bitcast(I32))
 
-        def load_scales(dst, src, q):
-            nc.sync.dma_start(
-                dst[32 * q : 32 * q + 4, :, :].bitcast(I32),
-                src[:, 0, 4 * q : 4 * q + 4, :].rearrange("e f n -> f e n").bitcast(I32),
-            )
+        def load_scales(tile, scales):
+            for q in range(QUADRANTS):
+                rows = scales[:, 0, 4 * q : 4 * q + 4, :].rearrange("e f n -> f e n")
+                nc.sync.dma_start(tile[32 * q : 32 * q + 4, :, :].bitcast(I32), rows.bitcast(I32))
 
-        def load_words(dst, src):
-            nc.sync.dma_start(dst[:].bitcast(I32), src.rearrange("e s p b -> p (e s) b").bitcast(I32))
+        load_dy(0)
+        for e in range(E):
+            nc.sync.dma_start(gates[e][:], gate[0:P, columns(e)])
+        load_dy(1)
+        load_a1(0)
+        load_dy(2)
+        load_dy(3)
+        load_a1(1)
+        load_words(w2_raw, w2_words)
+        load_a1(2)
+        load_a1(3)
+        load_a3(0)
+        load_scales(w2_scales_raw, w2_scales)
+        load_a3(1)
+        load_words(w1, w1_words)
+        load_words(w3, w3_words)
+        load_scales(w1_sc, w1_scales)
+        load_scales(w3_sc, w3_scales)
 
-        def permute_words():
-            nc.vector.tensor_copy(
-                w2[:].bitcast(U16).rearrange("p e (t m) -> p e t m", t=J),
-                w2_raw[:].bitcast(U16).rearrange("p e (m t) -> p e t m", t=J),
-            )
+        def in_planes(tile):
+            return tile[:].rearrange("p t (c i) -> p c t i", i=RUN)
 
-        def permute_scales():
-            nc.vector.tensor_copy(
-                w2s[:].rearrange("p e (t m) -> p e t m", t=J),
-                w2s_raw[:].rearrange("p e (m t) -> p e t m", t=J),
-            )
-
-        def slots(e):
-            return offsets[:, 32 * e : 32 * e + 32]
-
-        def by4(tile4):
-            return tile4[:].rearrange("p t (c i) -> p c t i", i=4)
-
-        def by4_out(tile4):
-            return tile4[:].rearrange("p (c i) t -> p c t i", i=4)
-
-        def gather(e, t):
-            nc.vector.tensor_tensor(g4[e][:, t, :], dy[t][:].indirect(slots(e)), gates[e][:], ALU.mult)
-
-        def sig(t):
-            nc.scalar.activation(sg[:, t, :], x1[:, t, :], ACT.Sigmoid)
-
-        def silu_neg(e, h):
-            nc.scalar.activation(
-                m[e][:, :, 256 * h : 256 * h + 256], x1[:, :, cols_of(e, h)], ACT.Silu, scale=-1.0
-            )
-
-        def silu(e):
-            o = keep.tile([P, J, C], F32, name=f"v_{e}", align_bytes=64)
-            nc.scalar.activation(o[:], x1[:, :, e * C : (e + 1) * C], ACT.Silu)
-            v[e] = o
-
-        def interleave(e):
-            o = keep.tile([P, C, J], BF16, name="g_bf", align_bytes=64)
-            nc.scalar.copy(by4_out(o), by4(g4[e]))
-            g_bf[e] = o
-
-        ps = {}
-
-        def make_p(e, h):
-            if e not in ps:
-                o = keep.tile([P, J, C], F32, name=f"p_{e}", align_bytes=64)
-                ps[e] = o
-            t, c = planes_of(h), slice(e * C, e * C + C)
-            if e == 1 and False:
-                nc.gpsimd.tensor_tensor(ps[e][:, t, :], sg[:, t, c], x3[:, t, c], ALU.mult)
-            else:
-                nc.vector.scalar_tensor_tensor(ps[e][:, t, :], sg[:, t, c], -1.0, x3[:, t, c], ALU.mult, ALU.mult)
-
-        def make_n(h):
-            c = slice(256 * h, 256 * h + 256)
-            nc.scalar.activation(m[1][:, :, c], m[1][:, :, c], ACT.Copy, bias=1.0, scale=-1.0)
-
-        def make_u(e, h):
-            c = slice(256 * h, 256 * h + 256)
-            if e == 1 and False:
-                nc.gpsimd.tensor_tensor(u[e][:, :, c], m[e][:, :, c], ps[e][:, :, c], ALU.mult)
-            else:
-                nc.vector.scalar_tensor_tensor(
-                    u[e][:, :, c], m[e][:, :, c], 1.0, ps[e][:, :, c], ALU.subtract, ALU.mult
-                )
-
-        daf = {}
-
-        def make_da_plane(label, e, t, factor):
-            if (label, e) not in daf:
-                name = f"daf{label}_{e}"
-                tag = {"daf3_1": "g4_0", "daf1_1": "g4_1"}.get(name, name)
-                o = keep.tile([P, J, C], F32, name=name, tag=tag, align_bytes=64)
-                daf[label, e] = o
-            nc.vector.tensor_tensor(daf[label, e][:, t, :], acc1[e, t][:], factor[:, t, :], ALU.mult)
-
-        def interleave_da(label, e):
-            o = keep.tile([P, C, J], BF16, name=f"da{label}_{e}", align_bytes=64)
-            nc.scalar.copy(by4_out(o), by4(daf[label, e]))
-            da[label, e] = o
+        def side_by_side(tile):
+            return tile[:].rearrange("p (c i) t -> p c t i", i=RUN)
 
         def quantise(src, label):
-            q = keep.tile([P, C], U32, name=f"codes_{label}", align_bytes=64)
-            z = keep.tile([P, C], U8, name=f"scales_{label}", align_bytes=64)
-            nc.vector.quantize_mx(out=q[:].bitcast(E5M2X4), scales=z[:], in_=src[:].rearrange("p c t -> p (c t)"))
-            codes[label], planes[label] = q, z
+            codes = keep.tile([P, C], U32, name=f"codes_{label}", align_bytes=64)
+            scales = keep.tile([P, C], U8, name=f"scales_{label}", align_bytes=64)
+            nc.vector.quantize_mx(
+                out=codes[:].bitcast(E5M2X4), scales=scales[:], in_=src[:].rearrange("p c t -> p (c t)")
+            )
+            return codes, scales
 
-        def first_product(e, t):
-            acc = psum.tile([P, C], F32, name=f"dh_acc{t}_{e}")
+        def multiply(acc, words, word_scales, e, m, operand, start, stop):
+            codes, scales = operand
             nc.tensor.matmul_mx(
                 out=acc[:],
-                lhsT=w2[:, e, 256 * t : 256 * t + 256].bitcast(E2M1X4),
-                lhsT_scale=w2s[:, e, 128 * t : 128 * t + 128],
-                rhs=codes[f"g{e}"][:].bitcast(E5M2X4),
-                rhs_scale=planes[f"g{e}"][:],
-                start=True,
-                stop=True,
+                lhsT=words[:, e, 2 * P * m : 2 * P * (m + 1)].bitcast(E2M1X4),
+                lhsT_scale=word_scales[:, e, P * m : P * (m + 1)],
+                rhs=codes[:].bitcast(E5M2X4),
+                rhs_scale=scales[:],
+                start=start,
+                stop=stop,
             )
-            acc1[e, t] = acc
 
-        def copy_dh(e, t):
-            nc.scalar.copy(dh[e][:, t, :], acc1[e, t][:])
+        def first_product(e, operand):
+            banks = []
+            for t in range(J):
+                acc = psum.tile([P, C], F32, name=f"dh_acc{t}_{e}")
+                multiply(acc, w2, w2_sc, e, t, operand, True, True)
+                banks.append(acc)
+            return banks
 
-        def make_da(label, e, factor):
-            o = keep.tile([P, C, J], BF16, name=f"da{label}_{e}", align_bytes=64)
-            nc.vector.tensor_tensor(by4_out(o), by4(dh[e]), by4(factor), ALU.mult)
-            da[label, e] = o
+        def copy_out(banks, e):
+            dh = keep.tile([P, J, C], F32, name=f"dh_{e}", align_bytes=64)
+            for t in range(J):
+                nc.scalar.copy(dh[:, t, :], banks[t][:])
+            return dh
 
-        def second_product(e, kt):
-            acc = psum.tile([P, C], F32, name=f"dx_acc{kt}_{e}", tag=f"dh_acc{kt + 2 * e}_0")
-            for n, (wt, ws, label) in enumerate(((w1, w1s, f"da1_{e}"), (w3, w3s, f"da3_{e}"))):
-                nc.tensor.matmul_mx(
-                    out=acc[:],
-                    lhsT=wt[:, e, 256 * kt : 256 * kt + 256].bitcast(E2M1X4),
-                    lhsT_scale=ws[:, e, 128 * kt : 128 * kt + 128],
-                    rhs=codes[label][:].bitcast(E5M2X4),
-                    rhs_scale=planes[label][:],
-                    start=(n == 0),
-                    stop=(n == 1),
-                )
-            acc2[e, kt] = acc
+        def silu(e):
+            value = keep.tile([P, J, C], F32, name=f"silu_{e}", align_bytes=64)
+            nc.scalar.activation(value[:], x1[:, :, columns(e)], ACT.Silu)
+            return value
 
-        def copy_dx(e, kt):
-            tag = f"dx{kt}_{e}"
-            o = keep.tile([P, C], F32, name=f"dx{kt}_{e}", tag=tag, align_bytes=64)
-            nc.scalar.copy(o[:], acc2[e, kt][:])
-            dxs[e, kt] = o
+        def gradient(dh, factor, label):
+            da = keep.tile([P, C, J], BF16, name=label, align_bytes=64)
+            nc.vector.tensor_tensor(side_by_side(da), in_planes(dh), in_planes(factor), ALU.mult)
+            return da
 
-        def scatter(e, kt):
-            nc.vector.tensor_copy(result[kt][:].indirect(slots(e)), dxs[e, kt][:])
+        def second_product(e, d1, d3):
+            dx = []
+            for kt in range(K // P):
+                acc = psum.tile([P, C], F32, name=f"dx_acc{kt}_{e}", tag=f"dh_acc{kt + 2 * e}_0")
+                multiply(acc, w1, w1_sc, e, kt, d1, True, False)
+                multiply(acc, w3, w3_sc, e, kt, d3, False, True)
+                dx.append(acc)
+            copies = []
+            for kt in range(K // P):
+                tile = keep.tile([P, C], F32, name=f"dx{kt}_{e}")
+                nc.scalar.copy(tile[:], dx[kt][:])
+                copies.append(tile)
+            return copies
 
-        def store(kt):
-            nc.sync.dma_start(out[kt * P : (kt + 1) * P, :], result[kt][:])
+        def scatter(e, kt, dx):
+            nc.vector.tensor_copy(result[kt][:].indirect(slots(e)), dx[kt][:])
 
+        g = []
+        for e in range(E):
+            tile = keep.tile([P, J, C], F32, name=f"g_{e}", align_bytes=64)
+            g.append(tile)
+        for t in range(J):
+            for e in range(E):
+                nc.vector.tensor_tensor(g[e][:, t, :], dy[t][:].indirect(slots(e)), gates[e][:], ALU.mult)
+
+        r = keep.tile([P, J, S], F32, name="r", align_bytes=64)
+        g_bf = []
+        for e in range(E):
+            tile = keep.tile([P, C, J], BF16, name=f"g_bf_{e}", align_bytes=64)
+            g_bf.append(tile)
+        for t in (0, 1):
+            nc.scalar.activation(r[:, t, :], x1[:, t, :], ACT.Sigmoid)
+        nc.scalar.copy(side_by_side(g_bf[0]), in_planes(g[0]))
+        for t in (2, 3):
+            nc.scalar.activation(r[:, t, :], x1[:, t, :], ACT.Sigmoid)
+
+        w2 = keep.tile([P, E, 2 * H], U8, name="w2", align_bytes=64)
+        w2_sc = keep.tile([P, E, H], U8, name="w2_sc", align_bytes=64)
+        nc.vector.tensor_copy(
+            w2[:].bitcast(U16).rearrange("p e (t m) -> p e t m", t=J),
+            w2_raw[:].bitcast(U16).rearrange("p e (m t) -> p e t m", t=J),
+        )
+        nc.vector.tensor_copy(side_by_side(g_bf[1]), in_planes(g[1]))
+        g_q = [quantise(g_bf[e], f"g_{e}") for e in range(E)]
+
+        minus_ra3 = keep.tile([P, J, S], F32, name="minus_ra3", align_bytes=64)
+        for half in range(2):
+            planes = slice(2 * half, 2 * half + 2)
+            nc.vector.scalar_tensor_tensor(
+                minus_ra3[:, planes, :], r[:, planes, :], -1.0, x3[:, planes, :], ALU.mult, ALU.mult
+            )
+        nc.vector.tensor_copy(
+            w2_sc[:].rearrange("p e (t m) -> p e t m", t=J),
+            w2_scales_raw[:].rearrange("p e (m t) -> p e t m", t=J),
+        )
+        silu_minus = []
+        for e in range(E):
+            tile = keep.tile([P, J, C], F32, name=f"silu_minus_{e}", align_bytes=64)
+            nc.scalar.activation(tile[:], x1[:, :, columns(e)], ACT.Silu, scale=-1.0)
+            silu_minus.append(tile)
+        banks = [first_product(e, g_q[e]) for e in range(E)]
+        u = []
+        for e in range(E):
+            tile = keep.tile([P, J, C], F32, name=f"u_{e}", align_bytes=64)
+            nc.vector.scalar_tensor_tensor(
+                tile[:], silu_minus[e][:], 1.0, minus_ra3[:, :, columns(e)], ALU.subtract, ALU.mult
+            )
+            u.append(tile)
+
+        dh0 = copy_out(banks[0], 0)
+        silu0 = silu(0)
+        da1_0 = gradient(dh0, u[0], "da1_0")
+        da3_0 = gradient(dh0, silu0, "da3_0")
+        dh1 = copy_out(banks[1], 1)
+        silu1 = silu(1)
+        d1_0 = quantise(da1_0, "da1_0")
+        d3_0 = quantise(da3_0, "da3_0")
+        da1_1 = gradient(dh1, u[1], "da1_1")
+        dx0 = second_product(0, d1_0, d3_0)
+        scatter(0, 0, dx0)
+        da3_1 = gradient(dh1, silu1, "da3_1")
+        d1_1 = quantise(da1_1, "da1_1")
+        d3_1 = quantise(da3_1, "da3_1")
+        scatter(0, 1, dx0)
+        dx1 = second_product(1, d1_1, d3_1)
         for kt in range(K // P):
-            nc.gpsimd.memset(result[kt][:], 0.0)
-
-        load_gate(0)
-        load_gate(1)
-        load_dy(2)
-        load_plane(x1, a1_rows, 0)
-        load_scales(w2s_raw, w2_scales, 0)
-        load_scales(w2s_raw, w2_scales, 1)
-        load_scales(w2s_raw, w2_scales, 2)
-        load_scales(w2s_raw, w2_scales, 3)
-        load_plane(x1, a1_rows, 3)
-        load_dy(3)
-        gather(0, 2)
-        sig(0)
-        gather(1, 2)
-        load_words(w2_raw, w2_words)
-        load_dy(1)
-        permute_scales()
-        load_plane(x1, a1_rows, 1)
-        gather(1, 3)
-        sig(3)
-        load_plane(x1, a1_rows, 2)
-        permute_words()
-        load_dy(0)
-        gather(0, 3)
-        load_half(x3, a3_rows, 1)
-        gather(1, 1)
-        sig(1)
-        sig(2)
-        gather(0, 1)
-        load_words(w1, w1_words)
-        load_half(x3, a3_rows, 0)
-        silu_neg(1, 0)
-        gather(0, 0)
-        gather(1, 0)
-        load_words(w3, w3_words)
-        make_p(0, 1)
-        silu_neg(1, 1)
-        make_p(1, 1)
-        interleave(0)
-        make_p(0, 0)
-        load_scales(w1s, w1_scales, 0)
-        load_scales(w1s, w1_scales, 1)
-        load_scales(w1s, w1_scales, 2)
-        load_scales(w1s, w1_scales, 3)
-        load_scales(w3s, w3_scales, 0)
-        load_scales(w3s, w3_scales, 1)
-        load_scales(w3s, w3_scales, 2)
-        load_scales(w3s, w3_scales, 3)
-        make_p(1, 0)
-        silu_neg(0, 0)
-        quantise(g_bf[0], "g0")
-        silu_neg(0, 1)
-        make_u(1, 1)
-        first_product(0, 2)
-        first_product(0, 3)
-        interleave(1)
-        first_product(0, 1)
-        first_product(0, 0)
-        make_u(1, 0)
-        make_u(0, 0)
-        copy_dh(0, 3)
-        quantise(g_bf[1], "g1")
-        copy_dh(0, 2)
-        copy_dh(0, 0)
-        make_u(0, 1)
-        first_product(1, 2)
-        first_product(1, 0)
-        copy_dh(0, 1)
-        first_product(1, 1)
-        first_product(1, 3)
-        silu(0)
-        make_da("1", 0, u[0])
-        copy_dh(1, 0)
-        make_da("3", 0, v[0])
-        copy_dh(1, 1)
-        copy_dh(1, 2)
-        copy_dh(1, 3)
-        silu(1)
-        quantise(da["1", 0], "da1_0")
-        quantise(da["3", 0], "da3_0")
-        make_da("1", 1, u[1])
-        second_product(0, 0)
-        second_product(0, 1)
-        copy_dx(0, 0)
-        copy_dx(0, 1)
-        make_da("3", 1, v[1])
-        scatter(0, 1)
-        quantise(da["3", 1], "da3_1")
-        quantise(da["1", 1], "da1_1")
-        scatter(0, 0)
-        second_product(1, 1)
-        second_product(1, 0)
-        copy_dx(1, 1)
-        copy_dx(1, 0)
-        scatter(1, 1)
-        scatter(1, 0)
-        store(1)
-        store(0)
+            scatter(1, kt, dx1)
+            nc.sync.dma_start(out[kt * P : (kt + 1) * P, :], result[kt][:])

from contextlib import ExitStack

import concourse.mybir as mybir

K, T, E, C, H, N = 256, 1280, 2, 512, 512, 512
S = E * C

F32 = mybir.dt.float32
BF16 = mybir.dt.bfloat16
U32 = mybir.dt.uint32
I32 = mybir.dt.int32
U16 = mybir.dt.uint16
U8 = mybir.dt.uint8
E5M2X4 = mybir.dt.float8_e5m2_x4
E2M1X4 = mybir.dt.float4_e2m1fn_x4
ACT = mybir.ActivationFunctionType
ALU = mybir.AluOpType

P = 128
J = 4
LIST_COLS = C // 16
QUADRANTS = 4
RUN = 4

FLOPS = 2 * S * (N * H + 2 * H * K)


def tile_moe_bdx_glu_silu_kernel(
    tc, dyT, a1, a3, w2_words, w2_scales, w1_words, w1_scales, w3_words, w3_scales, gate, offs, out
):
    nc = tc.nc
    with ExitStack() as ctx:
        lists = ctx.enter_context(tc.tile_pool(name="lists", bufs=1))
        keep = ctx.enter_context(tc.tile_pool(name="keep", bufs=1))
        psum = ctx.enter_context(tc.psum_pool(name="psum", bufs=1))

        offsets = lists.tile([P, S // 16], U16, name="offsets")
        nc.sync.dma_start(offsets[:], offs)

        def slots(e):
            return offsets[:, e * LIST_COLS : (e + 1) * LIST_COLS]

        def columns(e):
            return slice(e * C, (e + 1) * C)

        w2_scales_raw = keep.tile([P, E, H], U8, name="w2_scales_raw", align_bytes=64)
        w1_sc = keep.tile([P, E, K], U8, name="w1_sc", align_bytes=64)
        w3_sc = keep.tile([P, E, K], U8, name="w3_sc", align_bytes=64)
        for scale_tile in (w2_scales_raw, w1_sc, w3_sc):
            nc.gpsimd.memset(scale_tile[:].bitcast(I32), 0)

        result = []
        for kt in range(K // P):
            tile = keep.tile([P, T], F32, name=f"result{kt}")
            nc.gpsimd.memset(tile[:], 0.0)
            result.append(tile)

        dy, gates = [], []
        for t in range(J):
            tile = keep.tile([P, T], F32, name=f"dy{t}")
            dy.append(tile)
        for e in range(E):
            tile = keep.tile([P, C], F32, name=f"gate{e}")
            gates.append(tile)
        x1 = keep.tile([P, J, S], F32, name="x1", align_bytes=64)
        x3 = keep.tile([P, J, S], F32, name="x3", align_bytes=64)
        w2_raw = keep.tile([P, E, 2 * H], U8, name="w2_raw", align_bytes=64)
        w1 = keep.tile([P, E, 2 * K], U8, name="w1", align_bytes=64)
        w3 = keep.tile([P, E, 2 * K], U8, name="w3", align_bytes=64)
        dy_rows = dyT.rearrange("(p t) w -> p t w", t=J)
        a1_rows = a1.rearrange("(p t) c -> p t c", t=J)
        a3_rows = a3.rearrange("(p t) c -> p t c", t=J)

        def load_dy(t):
            nc.sync.dma_start(dy[t][:], dy_rows[:, t, :])

        def load_a1(t):
            nc.sync.dma_start(x1[:, t, :], a1_rows[:, t, :])

        def load_a3(half):
            planes = slice(2 * half, 2 * half + 2)
            nc.sync.dma_start(x3[:, planes, :], a3_rows[:, planes, :])

        def load_words(tile, words):
            nc.sync.dma_start(tile[:].bitcast(I32), words.rearrange("e s p b -> p (e s) b").bitcast(I32))

        def load_scales(tile, scales):
            for q in range(QUADRANTS):
                rows = scales[:, 0, 4 * q : 4 * q + 4, :].rearrange("e f n -> f e n")
                nc.sync.dma_start(tile[32 * q : 32 * q + 4, :, :].bitcast(I32), rows.bitcast(I32))

        load_dy(0)
        for e in range(E):
            nc.sync.dma_start(gates[e][:], gate[0:P, columns(e)])
        load_dy(1)
        load_a1(0)
        load_dy(2)
        load_dy(3)
        load_a1(1)
        load_words(w2_raw, w2_words)
        load_a1(2)
        load_a1(3)
        load_a3(0)
        load_scales(w2_scales_raw, w2_scales)
        load_a3(1)
        load_words(w1, w1_words)
        load_words(w3, w3_words)
        load_scales(w1_sc, w1_scales)
        load_scales(w3_sc, w3_scales)

        def in_planes(tile):
            return tile[:].rearrange("p t (c i) -> p c t i", i=RUN)

        def side_by_side(tile):
            return tile[:].rearrange("p (c i) t -> p c t i", i=RUN)

        def quantise(src, label):
            codes = keep.tile([P, C], U32, name=f"codes_{label}", align_bytes=64)
            scales = keep.tile([P, C], U8, name=f"scales_{label}", align_bytes=64)
            nc.vector.quantize_mx(
                out=codes[:].bitcast(E5M2X4), scales=scales[:], in_=src[:].rearrange("p c t -> p (c t)")
            )
            return codes, scales

        def multiply(acc, words, word_scales, e, m, operand, start, stop):
            codes, scales = operand
            nc.tensor.matmul_mx(
                out=acc[:],
                lhsT=words[:, e, 2 * P * m : 2 * P * (m + 1)].bitcast(E2M1X4),
                lhsT_scale=word_scales[:, e, P * m : P * (m + 1)],
                rhs=codes[:].bitcast(E5M2X4),
                rhs_scale=scales[:],
                start=start,
                stop=stop,
            )

        def first_product(e, operand):
            banks = []
            for t in range(J):
                acc = psum.tile([P, C], F32, name=f"dh_acc{t}_{e}")
                multiply(acc, w2, w2_sc, e, t, operand, True, True)
                banks.append(acc)
            return banks

        def copy_out(banks, e):
            dh = keep.tile([P, J, C], F32, name=f"dh_{e}", align_bytes=64)
            for t in range(J):
                nc.scalar.copy(dh[:, t, :], banks[t][:])
            return dh

        def silu(e):
            value = keep.tile([P, J, C], F32, name=f"silu_{e}", align_bytes=64)
            nc.scalar.activation(value[:], x1[:, :, columns(e)], ACT.Silu)
            return value

        def gradient(dh, factor, label):
            da = keep.tile([P, C, J], BF16, name=label, align_bytes=64)
            nc.vector.tensor_tensor(side_by_side(da), in_planes(dh), in_planes(factor), ALU.mult)
            return da

        def second_product(e, d1, d3):
            dx = []
            for kt in range(K // P):
                acc = psum.tile([P, C], F32, name=f"dx_acc{kt}_{e}", tag=f"dh_acc{kt + 2 * e}_0")
                multiply(acc, w1, w1_sc, e, kt, d1, True, False)
                multiply(acc, w3, w3_sc, e, kt, d3, False, True)
                dx.append(acc)
            copies = []
            for kt in range(K // P):
                tile = keep.tile([P, C], F32, name=f"dx{kt}_{e}")
                nc.scalar.copy(tile[:], dx[kt][:])
                copies.append(tile)
            return copies

        def scatter(e, kt, dx):
            nc.vector.tensor_copy(result[kt][:].indirect(slots(e)), dx[kt][:])

        g = []
        for e in range(E):
            tile = keep.tile([P, J, C], F32, name=f"g_{e}", align_bytes=64)
            g.append(tile)
        for t in range(J):
            for e in range(E):
                nc.vector.tensor_tensor(g[e][:, t, :], dy[t][:].indirect(slots(e)), gates[e][:], ALU.mult)

        r = keep.tile([P, J, S], F32, name="r", align_bytes=64)
        g_bf = []
        for e in range(E):
            tile = keep.tile([P, C, J], BF16, name=f"g_bf_{e}", align_bytes=64)
            g_bf.append(tile)
        for t in (0, 1):
            nc.scalar.activation(r[:, t, :], x1[:, t, :], ACT.Sigmoid)
        nc.scalar.copy(side_by_side(g_bf[0]), in_planes(g[0]))
        for t in (2, 3):
            nc.scalar.activation(r[:, t, :], x1[:, t, :], ACT.Sigmoid)

        w2 = keep.tile([P, E, 2 * H], U8, name="w2", align_bytes=64)
        w2_sc = keep.tile([P, E, H], U8, name="w2_sc", align_bytes=64)
        nc.vector.tensor_copy(
            w2[:].bitcast(U16).rearrange("p e (t m) -> p e t m", t=J),
            w2_raw[:].bitcast(U16).rearrange("p e (m t) -> p e t m", t=J),
        )
        nc.vector.tensor_copy(side_by_side(g_bf[1]), in_planes(g[1]))
        g_q = [quantise(g_bf[e], f"g_{e}") for e in range(E)]

        minus_ra3 = keep.tile([P, J, S], F32, name="minus_ra3", align_bytes=64)
        for half in range(2):
            planes = slice(2 * half, 2 * half + 2)
            nc.vector.scalar_tensor_tensor(
                minus_ra3[:, planes, :], r[:, planes, :], -1.0, x3[:, planes, :], ALU.mult, ALU.mult
            )
        nc.vector.tensor_copy(
            w2_sc[:].rearrange("p e (t m) -> p e t m", t=J),
            w2_scales_raw[:].rearrange("p e (m t) -> p e t m", t=J),
        )
        silu_minus = []
        for e in range(E):
            tile = keep.tile([P, J, C], F32, name=f"silu_minus_{e}", align_bytes=64)
            nc.scalar.activation(tile[:], x1[:, :, columns(e)], ACT.Silu, scale=-1.0)
            silu_minus.append(tile)
        banks = [first_product(e, g_q[e]) for e in range(E)]
        u = []
        for e in range(E):
            tile = keep.tile([P, J, C], F32, name=f"u_{e}", align_bytes=64)
            nc.vector.scalar_tensor_tensor(
                tile[:], silu_minus[e][:], 1.0, minus_ra3[:, :, columns(e)], ALU.subtract, ALU.mult
            )
            u.append(tile)

        dh0 = copy_out(banks[0], 0)
        silu0 = silu(0)
        da1_0 = gradient(dh0, u[0], "da1_0")
        da3_0 = gradient(dh0, silu0, "da3_0")
        dh1 = copy_out(banks[1], 1)
        silu1 = silu(1)
        d1_0 = quantise(da1_0, "da1_0")
        d3_0 = quantise(da3_0, "da3_0")
        da1_1 = gradient(dh1, u[1], "da1_1")
        dx0 = second_product(0, d1_0, d3_0)
        scatter(0, 0, dx0)
        da3_1 = gradient(dh1, silu1, "da3_1")
        d1_1 = quantise(da1_1, "da1_1")
        d3_1 = quantise(da3_1, "da3_1")
        scatter(0, 1, dx0)
        dx1 = second_product(1, d1_1, d3_1)
        for kt in range(K // P):
            scatter(1, kt, dx1)
            nc.sync.dma_start(out[kt * P : (kt + 1) * P, :], result[kt][:])
